import numpy as np, ml_dtypes
CORES = [5,29,101,125,133,157,229,253]
N = 8
import mx_ref
BF = ml_dtypes.bfloat16
def gentries(a):
    return np.ascontiguousarray(a.reshape(8, 16, -1).transpose(0, 2, 1)).reshape(8, -1)
def gtable(e):
    e = np.asarray(e); return np.ascontiguousarray(e.reshape(8, -1, 16).transpose(0, 2, 1)).reshape(128, -1).astype(np.int32)
def gcols(t, e):
    v = np.concatenate([t.reshape(8, 16, -1, 4), np.zeros((8, 16, 1, 4), BF)], axis=2)
    return np.ascontiguousarray(np.stack([v[g][:, e[g]] for g in range(8)])).reshape(128, -1)
def gpick(z, e):
    return np.concatenate([z[16 * g:16 * g + 16][:, e[g]] for g in range(8)])
def tile(rs):
    return np.stack(rs, axis=2).reshape(128, -1).astype(BF)
def pick(q, e):
    c = np.concatenate([q[0].reshape(128, -1, 4), np.zeros((128, 1, 4), np.uint8)], axis=1); s = np.concatenate([q[1], np.ones((16, 1), np.uint8)], axis=1)
    return (np.ascontiguousarray(c[:, e].reshape(128, -1)), np.ascontiguousarray(s[:, e]))
def join(*qs):
    return (np.concatenate([q[0] for q in qs], axis=1), np.concatenate([q[1] for q in qs], axis=1))
def put(q, e, v):
    c, s = q[0].reshape(128, -1, 4).copy(), q[1].copy(); c[:, e] = v[0].reshape(128, -1, 4); s[:, e] = v[1]
    return (c.reshape(128, -1), s)
def pk(c, s):
    return (np.ascontiguousarray(c), mx_ref.live(s))
def emit(q):
    return q[0], q[1]
def packed(v, rng):
    q = [mx_ref.quantize(np.ascontiguousarray(v[r])) for r in range(N)]
    return np.stack([a for a, b in q]), np.stack([mx_ref.plane(b, rng) for a, b in q])
def values_of_codes():
    e, c = np.zeros((128, 128, 4), np.float32), np.zeros((128, 2, 4), np.uint8)
    e[np.arange(128), np.arange(128), 0] = 1
    c[:127, :, 0] = np.arange(256).reshape(2, 128).T[:127]
    return mx_ref.matmul(mx_ref.quantize(e.reshape(128, 512).astype(BF)), (c.reshape(128, 8), np.full((16, 2), 127, np.uint8))).T.reshape(-1).astype(np.float64)
CODE_VALUE, SCALE_VALUE = values_of_codes(), 2.0 ** (np.arange(256) - 127.0)
def decode(q):
    return (CODE_VALUE[q[0]].reshape(16, 8, -1, 4) * SCALE_VALUE[q[1]][:, None, :, None] + 0.0).reshape(128, -1).astype(np.float32)
def f(rng, *shape):
    return mx_ref.flush((rng.standard_normal(shape, dtype=np.float32) * np.exp2(rng.integers(-2, 3, shape[:-1] + (1,)))).astype(BF))
def wide(rng, *shape, cols=0):
    v = rng.standard_normal(shape, dtype=np.float32) * np.exp2(rng.integers(-12, 13, shape)).astype(np.float32)
    if cols: v *= np.repeat(np.exp2(rng.integers(-cols, cols + 1, shape[:-2] + (1, shape[-1] // 4))) * (rng.random(shape[:-2] + (1, shape[-1] // 4)) > 0.0625), 4, axis=-1).astype(np.float32)
    return mx_ref.flush(v.astype(BF))
C, R = 288, 3
DECIDE = [0, 1, 2, 16, 32, 48, 64, 80, 96, 112]
def big(a):
    a = a.astype(np.float32)
    a[np.abs(a) < np.float32(2.0 ** -16)] = 0
    return a
def numbers_of(rng):
    return big(f(rng, N, 128, 4 * C)).reshape(N, 8, 16, C, 4), f(rng, N, 128, 512).astype(np.float32).reshape(N, 8, 16, 128, 4), f(rng, N, 128, 512).astype(np.float32).reshape(N, 8, 16, 128, 4)
def layers(rng, still=[]):
    w = np.clip(big(f(rng, N, 128, 2048)), -1, 1).reshape(N, 8, 16, 4, 8, 16, 4)
    w[:, :, still] = 0
    w[:, :, :, :, :, still] = 0
    return w
def inputs(rng, x, u, v, p, w):
    x, u, v, w = [np.ascontiguousarray(a).astype(np.float32).reshape(N, 128, -1).astype(BF) for a in (x, u, v, w)]
    c, s = packed(w, rng)
    return {"x": x, "u": u, "v": v, "p": np.stack([gtable(p[r]) for r in range(N)]), "wc": c, "ws": s}
def pointers(rng):
    return rng.integers(0, C, (N, 8, C))
def setup_inputs(rng):
    x, u, v = numbers_of(rng)
    return inputs(rng, x, u, v, pointers(rng), layers(rng))
def setup_inputs_ties(rng):
    x, u, v = numbers_of(rng)
    o = rng.permutation(N)
    k = rng.integers(0, 3, (N, 8, C, 4))
    k[:, :, :, 2] -= 1
    k[:, :, :, 3] = 0
    k[o[1], :, :, 2] = 1
    x[:, :, 0] = k
    h = np.ones(N)
    h[o[0]] = 0
    h[o[1]] = -1
    u[:, :, :, DECIDE] = 0
    for g in range(8): u[:, g, 0, 16 * g, 0] = h
    u[:, 0, 0, 1, 1] = 1
    u[:, 0, 0, 2, 2] = 1
    u[o[2], :, :, 1] = 0
    u[o[3], :, :, 2] = 0
    return inputs(rng, x, u, v, pointers(rng), layers(rng, [0]))
def setup_inputs_near(rng):
    x, u, v = numbers_of(rng)
    hold = [0, 1] + [i for i in range(8, 16)]
    x[:, :, hold] = 0
    u[:, :, :, DECIDE] = 0
    o = rng.permutation(N) % 4
    e = 2.0 ** -30
    for r in range(N):
        k = 1.0 if o[r] == 0 else e
        s, n = rng.integers(0, 16, (8, C)), rng.integers(0, 16, C)
        c, m = rng.integers(0, 2, C) * 2.0 - 1.0, rng.integers(0, 2, C) * 2.0 - 1.0
        z = rng.integers(-1, 2, C)
        x[r, :, 8] = ((s[:, :, None] >> np.arange(4)) & 1) * np.exp2(np.arange(4) - 23.0)
        x[r, 0, 9] = ((n[:, None] >> np.arange(4)) & 1) * np.exp2(np.arange(4) - 23.0)
        if o[r] < 2:
            x[r, :, 0, :, 0] = c
            x[r, :, 11, :, 0] = 2.0 ** -10
            x[r, 0, 1, :, 0] = m
            x[r, 0, 12, :, 0] = 2.0 ** -10
            x[r, 1, 9, :, 0] = z * 2.0 ** -23
            u[r, 0, 1, 1, 0] = k
            u[r, 0, 12, 1, 0] = k
            u[r, 1, 9, 2, 0] = k
        elif o[r] == 2:
            x[r, :, 0, :, 0] = np.where(c < 0, -1.0, 0.0)
            x[r, 0, 1, :, 0] = np.where(rng.permutation(C) % 8 == 0, m, 0.0)
            x[r, 1, 13, :, 0] = z * e
            u[r, 0, 1, 1, 0] = 1
            u[r, 1, 13, 2, 0] = e
        else:
            x[r, :, 10, :, 0] = rng.integers(1, 3, (8, C)) * c * np.where(np.arange(8) < 4, e, 1.125 * e)[:, None]
            x[r, 0, 14, :, 0] = rng.integers(-2, 3, C) * e
            x[r, 1, 13, :, 0] = z * 1.125 * e
            x[r, 1, 14, :, 0] = (0 - z) * 1.25 * e
            u[r, 0, 14, 1, 0] = e
            u[r, 1, 13, 2, 0] = 1.125 * e
            u[r, 1, 14, 2, 0] = e
        if o[r] < 3: u[r, 0, 9, 1] = k
        far = rng.permutation(8)
        for g in range(8):
            if o[r] < 2:
                u[r, g, 0, 16 * g, 0] = k
                u[r, g, 11, 16 * g, 0] = k
            if o[r] == 2 and g in far[:2]: u[r, g, 0, 16 * g, 0] = 1
            if o[r] < 3: u[r, g, 8, 16 * g] = k
            else: u[r, g, 10, 16 * g, 0] = 1.25 * e if g < 4 else 1.125 * e
    return inputs(rng, x, u, v, pointers(rng), layers(rng, hold))
def setup_inputs_late(rng):
    x, u, v = numbers_of(rng)
    x[:, :, 0] = (rng.permutation(N) % 2 * 0.0625)[:, None, None, None]
    u[:, :, :, DECIDE] = 0
    for g in range(8): u[:, g, 0, 16 * g, 0] = 1
    u[:, 0, 0, 1, 1] = 1
    u[:, 0, 0, 2, 2] = 1
    return inputs(rng, x, u, v, pointers(rng), layers(rng))
def setup_inputs_ends(rng):
    x, u, v = numbers_of(rng)
    o, h = rng.permutation(N), rng.permutation(8)
    p = pointers(rng)
    x[:] = np.where(rng.random((N, 8, 1, C, 1)) < 0.5, 0.875, 1.0) * 2.0 ** 25
    v[:] = (rng.integers(0, 2, (N, 1, 1, 128, 1)) * 2.0 - 1.0) * 2.0 ** 30
    u[:, :, :, DECIDE] = 2.0 ** 30
    for g in range(8): u[:, g, :, 16 * g] = 2.0 ** 29
    u[:, :, :, 2] = 0
    u[:, 0, :, 2] = 2.0 ** 30
    u[:, 1, :, 2] = -2.0 ** 30
    p[o[0]] = C - 1
    x[o[0], :, :, :C - 1] = 2.0 ** -30
    u[o[0], :, :, 2] = -2.0 ** 30
    p[o[1]] = 0
    x[o[1]] = 2.0 ** 25
    u[o[1], :, :, ::16] = 2.0 ** 30
    u[o[1], :, :, 2] = 2.0 ** 30
    p[o[2], h[:4]] = C - 1
    p[o[2], h[4:]] = 0
    p[o[2], 0] = rng.permutation(C)
    x[o[2], :, :, 1 + rng.permutation(C - 2)[:C // 2]] = 2.0 ** -30
    u[o[2], :, :, ::16] = -2.0 ** 30
    u[o[2], 0, :, 112] = -2.0 ** 29
    u[o[2], :, :, 1] *= -1
    u[o[2], :, :, 2] = 2.0 ** 30
    for g in h[:4]: u[o[3], :, :, 16 * g] *= -1
    u[o[3], :, :, 3:16] = 2.0 ** -30
    v[o[3]] = 2.0 ** -30
    return inputs(rng, x, u, v, p, np.ones((N, 128, 2048)))
def setup_inputs_spread(rng):
    x, u, v = numbers_of(rng)
    return inputs(rng, big(wide(rng, N, 128, 4 * C, cols=6)), u, v, pointers(rng), layers(rng))
def check_inputs(d):
    b = []
    for k, top in (("x", 2.0 ** 25), ("u", 2.0 ** 30), ("v", 2.0 ** 30)):
        a = np.abs(d[k].astype(np.float32))
        if not (np.isfinite(a).all() and ((a == 0) | (a >= 2.0 ** -30) & (a <= top)).all()): b.append("a value of " + k)
    if not ((d["p"] >= 0) & (d["p"] < C)).all(): b.append("an entry of p")
    none, least, most = [emit(mx_ref.quantize(np.full((128, 16), k, np.float32).astype(BF)))[1][0, 0] for k in (0.0, 2.0 ** -30, 1.0)]
    for r in range(N):
        if ((d["wc"][r] == 0x7F) | (d["wc"][r] == 0xFF)).any(): b.append("wc: a code that is no number")
        s = mx_ref.live(d["ws"][r])
        if ((s != none) & ((s < least) | (s > most))).any(): b.append("ws: a scale out of range")
        with np.errstate(all="ignore"):
            if not (np.abs(decode(pk(d["wc"][r], d["ws"][r]))) <= 1).all(): b.append("a number of W beyond 1 in size")
    return b
def reference(x, u, v, p, wc, ws):
    qu = [mx_ref.quantize(u[r]) for r in range(N)]
    lay = [pk(wc[r], ws[r]) for r in range(N)]
    first = np.stack([gentries(p[r]) for r in range(N)])
    ptr = first.copy()
    now = [x[r] for r in range(N)]
    g, j = np.arange(8)[:, None], np.arange(C)
    for t in range(R):
        sent, via = [], []
        for r in range(N):
            s = mx_ref.matmul(qu[r], mx_ref.quantize(now[r])) + np.float32(0.0)
            level = np.argmax(s[::16], axis=0)
            o = np.argsort(-s[1], kind="stable")
            c = np.zeros(C, np.int64)
            c[o] = np.roll(o, -1)
            call = s[2] > 0
            new = np.where((g < level) & call, ptr[r][:, c], ptr[r])
            new = np.where(g == level, np.where(call, j, first[r]), new)
            ptr[r] = new
            via.append(new[:, c])
            sent.append(mx_ref.quantize(gcols(now[r], new)))
        for r in range(N):
            q = sent[(r - 1 - t) % N]
            h = [mx_ref.matmul(pick(lay[r], np.arange(128 * b, 128 * b + 128)), q) * np.float32(0.00390625) for b in range(4)]
            now[r] = tile([gpick(h[b], via[r]) + now[r][:, b::4].astype(np.float32) for b in range(4)])
    y, op = np.zeros((N, 128, C), np.float32), np.zeros((N, 8, C), np.float32)
    oc, osc = np.zeros((N, 128, 4 * C), np.uint8), np.zeros((N, 16, C), np.uint8)
    for r in range(N):
        q = mx_ref.quantize(now[r])
        y[r] = mx_ref.matmul(mx_ref.quantize(v[r]), q)
        op[r] = ptr[r]
        oc[r], osc[r] = emit(q)
    return {"y": y, "op": op, "oc": oc, "osc": osc}

import numpy as np
from concourse.bass import DstId, RemoteDMATransfer
from concourse.mybir import dt, AluOpType as A, AxisListType, ActivationFunctionType as F

C, R = 288, 3
CA = 160
SORT, OWN, NUM, INP, WEND = 0, 304, 592, 880, 1168

SCRATCH = {
    "ut": ("sbuf", [128, 512], "bfloat16"), "vt": ("sbuf", [128, 512], "bfloat16"),
    "uc": ("sbuf", [128, 128], "float8_e4m3fn_x4"), "us": ("sbuf", [128, 128], "uint8"),
    "vc": ("sbuf", [128, 128], "float8_e4m3fn_x4"), "vs": ("sbuf", [128, 128], "uint8"),
    "urc": ("sbuf", [128, 128], "float8_e4m3fn_x4"), "urs": ("sbuf", [128, 128], "uint8"),
    "wcb": ("sbuf", [128, 512], "float8_e4m3fn_x4"), "wsb": ("sbuf", [128, 512], "uint8"),
    "pi": ("sbuf", [128, 18], "int32"), "pl": ("sbuf", [128, 18], "uint16"),
    "one16": ("sbuf", [128, 8], "uint16"),
    "win0": ("sbuf", [128, WEND], "float32"), "win1": ("sbuf", [128, WEND], "float32"),
    "ones": ("sbuf", [128, C], "bfloat16"), "kt": ("sbuf", [128, 3 * C], "bfloat16"),
    "gi": ("sbuf", [128, 2], "int32"), "pmi": ("sbuf", [128, 2], "int32"), "ggi": ("sbuf", [128, 2], "int32"),
    "pm": ("sbuf", [128, 2], "float32"), "bias": ("sbuf", [128, 4], "float32"),
    "ni": ("sbuf", [128, 32], "int32"), "nj": ("sbuf", [128, 32], "int32"), "neg": ("sbuf", [128, 32], "float32"),
    "ti": ("sbuf", [128, C], "int32"), "tj": ("sbuf", [128, C], "int32"),
    "rm": ("sbuf", [128, 96], "float32"),
    "ka": ("sbuf", [128, C], "float32"), "kb": ("sbuf", [128, C], "float32"),
    "kd": ("sbuf", [128, C], "float32"), "qi": ("sbuf", [128, 18], "int32"),
    "low": ("sbuf", [128, 8], "float32"),
    "comp": ("sbuf", [128, 72], "float32"), "m4": ("sbuf", [128, 72], "float32"), "rest": ("sbuf", [128, 72], "float32"),
    "pmx": ("sbuf", [128, 24], "float32"), "jk": ("sbuf", [128, 24], "float32"),
    "lv": ("sbuf", [128, 3], "float32"), "t1": ("sbuf", [128, 3], "float32"), "t2": ("sbuf", [128, 3], "float32"),
    "t3": ("sbuf", [128, 3], "float32"), "zz": ("sbuf", [128, 3], "float32"), "wv": ("sbuf", [128, 3], "float32"),
    "sneg": ("sbuf", [128, 3], "float32"), "cl": ("sbuf", [128, 3], "float32"), "acc": ("sbuf", [128, 3], "float32"),
    "sg": ("sbuf", [128, 3 * C], "bfloat16"), "eq": ("sbuf", [128, 3 * C], "bfloat16"), "fs": ("sbuf", [128, 3 * C], "float16"),
    "bm": ("sbuf", [128, 96], "float32"), "bt": ("sbuf", [128, 96], "float32"), "sc": ("sbuf", [128, 96], "float32"),
    "glf": ("sbuf", [128, 18], "float32"), "gli": ("sbuf", [128, 18], "int32"), "rk": ("sbuf", [128, 18], "int32"),
    "r16": ("sbuf", [128, 18], "uint16"), "rn16": ("sbuf", [128, 18], "uint16"),
    "hh": ("sbuf", [128, 18], "float32"), "ff": ("sbuf", [128, 18], "float32"), "fm": ("sbuf", [128, 18], "float32"),
    "offd": ("sbuf", [128, 18], "uint16"), "offz": ("sbuf", [128, 18], "uint16"), "offv": ("sbuf", [128, 18], "uint16"),
    "sk": ("sbuf", [128, C], "float32"), "sk2": ("sbuf", [128, C], "float32"), "via": ("sbuf", [128, C], "float32"),
    "yt": ("sbuf", [128, C], "float32"), "opf": ("sbuf", [128, C], "float32"),
    "rc0": ("sbuf", [128, CA], "float8_e4m3fn_x4"), "rs0": ("sbuf", [128, C], "uint8"),
    "rc2": ("sbuf", [128, CA], "float8_e4m3fn_x4"), "rs2": ("sbuf", [128, C], "uint8"),
    "pc": ("psum", [128, 1536], "float32"), "pf": ("psum", [128, 512], "float32"),
    "pv": ("psum", [128, 512], "float32"), "ph": ("psum", [128, 1536], "float32"),
}
for _t in range(R + 1):
    _n = 320 if _t < R else C
    SCRATCH["xt%d" % _t] = ("sbuf", [128, 4 * _n], "bfloat16")
    SCRATCH["xc%d" % _t] = ("sbuf", [128, _n], "float8_e4m3fn_x4")
    SCRATCH["xs%d" % _t] = ("sbuf", [128, _n], "uint8")
for _t in range(R):
    SCRATCH["xp%d" % _t] = ("sbuf", [128, 4 * C], "bfloat16")
    SCRATCH["zt%d" % _t] = ("sbuf", [128, 4 * C], "bfloat16")
    SCRATCH["zc%d" % _t] = ("sbuf", [128, C], "float8_e4m3fn_x4")
    SCRATCH["zs%d" % _t] = ("sbuf", [128, C], "uint8")
    SCRATCH["lc%d" % _t] = ("sbuf", [128, C], "float8_e4m3fn_x4")
    SCRATCH["ls%d" % _t] = ("sbuf", [128, C], "uint8")
    SCRATCH["hs%d" % _t] = ("sbuf", [128, 4 * C], "float32")
SEMAPHORES = ["sv", "ss", "st", "sg", "out", "in0", "in2"] + ["la%d" % t for t in range(R)] + ["lb%d" % t for t in range(R)] + ["lp%d" % t for t in range(R)] \
    + ["dx", "du", "dp", "dw", "dws", "dv", "oy", "oy2", "oop", "oc", "os0", "os1", "os2", "os3"]


def relays(own, dst, topo):
    if topo.may_write(own, dst):
        return None
    c = [k for k in topo.cores_of(own) if k != own and topo.may_write(k, dst)]
    near = [k for k in c if topo.die(k) == topo.die(own)]
    far = [k for k in c if topo.die(k) != topo.die(own)]
    return [far[0], near[0], near[1]]


def send(g, T, topo, src, dst, out, in_, sem):
    rid, pid = topo.addr(dst, src)
    g.remote_dma(out, in_, T.sem[sem], T.sem.out, pid, rid, topo.mask(src, dst))
    return len(topo.engines(src, dst))


def bits(view):
    return view.bitcast(dt.uint8)


PIECE = [(0, CA), (CA, C)]
LAND = ["la", "lb", "lp"]


def rank_program(g, core, T, topo):
    if T.rank_of(core) is None:
        hand_on(g, core, T, topo)
    else:
        work(g, core, T, topo)


def hand_on(g, core, T, topo):
    own = [k for k in T.cores if k in topo.cores_of(core)]
    if not own:
        return
    own, n, total = own[0], len(T.cores), 0
    for t in range(R):
        dst = T.cores[(T.rank_of(own) + 1 + t) % n]
        rel = relays(own, dst, topo)
        if rel is None or core not in rel:
            continue
        k = rel.index(core)
        g.wait_ge(T.sem["in%d" % t], len(topo.engines(own, core)))
        if k < 2:
            a, b = PIECE[k]
            total += send(g, T, topo, core, dst, bits(T["lc%d" % t][:, a:b]), bits(T["rc%d" % t][:, 0:b - a]), LAND[k] + str(t))
        else:
            total += send(g, T, topo, core, dst, T["ls%d" % t][:, :], T["rs%d" % t][:, :], LAND[k] + str(t))
    if total:
        g.wait_ge(T.sem.out, total)


def work(g, core, T, topo):
    rank, n = T.rank_of(core), len(T.cores)
    Q = {"v": g.vector, "s": g.scalar, "t": g.tensor, "g": g, "y": g.sync}
    S = {"v": "sv", "s": "ss", "t": "st", "g": "sg"}
    cnt = {"sv": 0, "ss": 0, "st": 0, "sg": 0}
    waited, acc, other = {}, {}, []
    PS = ("pc", "pf", "pv", "ph")

    def norm(x):
        return (x, 0, 1 << 20) if isinstance(x, str) else x

    def need(e, sem, val):
        if waited.get((e, sem), 0) < val:
            waited[(e, sem)] = val
            Q[e].wait_ge(T.sem[sem], val)

    def order(e, eng, reads, writes):
        want = {}
        for w, lst in ((False, reads), (True, writes)):
            for key, lo, hi in map(norm, lst):
                for b in acc.get(key, []):
                    if b[0] >= hi or b[1] <= lo:
                        continue
                    same = b[5] == eng
                    if not (w or b[2]) and (same or key not in PS):
                        continue
                    if same and w and not b[2]:
                        continue
                    want[b[3]] = max(want.get(b[3], 0), b[4])
        for sem in sorted(want):
            need(e, sem, want[sem])

    def note(eng, sem, val, reads, writes):
        for w, lst in ((False, reads), (True, writes)):
            for key, lo, hi in map(norm, lst):
                keep = []
                for b in acc.get(key, []):
                    inside = lo <= b[0] and b[1] <= hi
                    if inside and (w or (b[5] == eng and not b[2])):
                        continue
                    keep.append(b)
                keep.append((lo, hi, w, sem, val, eng))
                acc[key] = keep

    def op(e, reads, writes, call, *args, **kw):
        order(e, e, reads, writes)
        sem = S[e]
        call(*args, **kw).then_inc(T.sem[sem], 1)
        cnt[sem] += 1
        note(e, sem, cnt[sem], reads, writes)

    def load(e, out, in_, sem, reads, writes):
        order(e, sem, reads, writes)
        Q[e].dma_start(out, in_).then_inc(T.sem[sem], 16)
        note(sem, sem, 16, reads, writes)
        other.append((sem, 16))

    def arrived(sem, num, writes):
        note(sem, sem, num, [], writes)
        other.append((sem, num))

    V, X = g.vector, g.scalar
    ts, tt, cp, act, scan = V.tensor_scalar, V.tensor_tensor, V.tensor_copy, X.activation, V.tensor_tensor_scan

    load("y", T.xt0[:, 0:4 * C], T.x[:, :], "dx", [], [("xt0", 0, 4)])
    load("s", T.ut[:, :], T.u[:, :], "du", [], ["ut"])
    load("s", T.pi[:, :], T.p[:, :], "dp", [], ["pi"])
    load("y", bits(T.wcb[:, :]), T.wc[:, :], "dw", [], ["wcb"])
    load("y", T.wsb[:, :], T.ws[:, :], "dws", [], ["wsb"])
    load("y", T.vt[:, :], T.v[:, :], "dv", [], ["vt"])

    op("v", [], [("xt0", 4, 5)], V.memset, T.xt0[:, 4 * C:1280], 0.0)
    op("v", [], ["one16"], V.memset, T.one16[:, :], 1)
    op("v", [], ["ones"], V.memset, T.ones[:, :], 1.0)
    op("g", [], ["gi"], g.iota, T.gi[:, 0:2], [[0, 2]], 0, 1)
    op("g", [], ["ti"], g.iota, T.ti[:, :], [[1, C]], 0, 0)
    op("g", [], ["ni"], g.iota, T.ni[:, :], [[1, 32]], 128, -1)
    op("g", [], ["qi"], g.iota, T.qi[:, :], [[16, 18]], OWN - 1 + 144, 0)
    op("g", [], [("w0", NUM, INP)], g.iota, T.win0[:, NUM:INP], [[1, C]], 1, 0, allow_small_or_imprecise_dtypes=True)
    for c in range(3):
        op("g", ["ones"], [("kt", c, c + 1)], g.affine_select, T.kt[:, C * c:C * c + C], T.ones[:, :], [[1, C]], A.not_equal, -1.0, -96 * c, -1)
    op("g", [], [("w1", NUM, INP)], g.iota, T.win1[:, NUM:INP], [[1, C]], 1, 0, allow_small_or_imprecise_dtypes=True)
    op("v", [], [("w0", SORT, OWN)], V.memset, T.win0[:, SORT:OWN], 1.0)
    op("v", [], [("w1", SORT, OWN)], V.memset, T.win1[:, SORT:OWN], 1.0)
    op("v", [], ["low"], V.memset, T.low[:, :], -1e29)
    for k, m in enumerate((0.0, -1.0, -2.0, 144.0)):
        op("v", [], [("m4", k, k + 1)], V.memset, T.m4[:, k:72:4], m)
    op("v", ["gi"], ["pmi"], ts, T.pmi[:, :], T.gi[:, :], 15, None, A.bitwise_and)
    op("v", ["gi"], ["ggi"], ts, T.ggi[:, :], T.gi[:, :], 4, None, A.arith_shift_right)
    op("v", ["ti"], ["tj"], ts, T.tj[:, :], T.ti[:, :], 15, None, A.bitwise_and)
    op("v", ["ni"], ["nj"], ts, T.nj[:, :], T.ni[:, :], 15, None, A.bitwise_and)
    op("v", ["pmi"], ["pm"], cp, T.pm[:, :], T.pmi[:, :])
    op("v", ["nj"], ["neg"], ts, T.neg[:, :], T.nj[:, :], 0, -1048576.0, A.is_gt, A.mult)
    op("v", ["tj"], ["rm"], ts, T.rm[:, :], T.tj[:, 0:96], 1.0, None, A.min)
    for k, (m, b) in enumerate(((1024.0, -7167.0), (1024.0, -8191.0), (-1024.0, -8191.0), (4096.0, 36864.0))):
        op("v", ["ggi"], [("bias", k, k + 1)], ts, T.bias[:, k:k + 1], T.ggi[:, 0:1], m, b, A.mult, A.add)

    def quantise(xc, xs, xt, a, b, name):
        op("v", [("x" + name, 0, 5)], [("q" + name, a, b)], V.quantize_mx, T[xc][:, a:b], T[xs][:, a:b], T[xt][:, 4 * a:4 * b])

    op("v", ["ut"], ["uc"], V.quantize_mx, T.uc[:, 0:128], T.us[:, 0:128], T.ut[:, 0:512])
    op("v", ["uc", "one16"], ["urc"], cp, T.urc[:, 0:128].bitcast(dt.uint32), T.uc[:, 0:128].bitcast(dt.uint32).indirect(T.one16[:, 0:8]))
    op("v", ["uc", "one16"], ["urs"], cp, T.urs[:, 0:128], T.us[:, 0:128].indirect(T.one16[:, 0:8]))
    quantise("xc0", "xs0", "xt0", 0, 320, "t0")

    def planes(t, b):
        op("s", [("xt%d" % t, b, b + 1)], [("xp%d" % t, b, b + 1)], act, T["xp%d" % t][:, C * b:C * b + C], T["xt%d" % t][:, b:4 * C:4], F.Copy)

    for b in range(4):
        planes(0, b)

    def later_constants():
        op("v", ["pi"], ["pl"], cp, T.pl[:, :], T.pi[:, :])
        op("v", ["pl", ("w0", NUM, INP)], [("w0", INP, WEND)], cp, T.win0[:, INP:WEND], T.win0[:, NUM:INP].indirect(T.pl[:, 0:18]))
        op("v", ["qi", "pm"], [("comp", 3, 4)], ts, T.comp[:, 3:72:4], T.qi[:, :], T.pm[:, 0:1], None, A.add)
        op("v", ["tj", "pm"], ["ka"], ts, T.ka[:, :], T.tj[:, :], T.pm[:, 0:1], 2.0 ** -20 - 1, A.is_lt, A.mult)
        op("v", ["tj", "pm"], ["kb"], ts, T.kb[:, :], T.tj[:, :], T.pm[:, 0:1], 1023.0, A.is_equal, A.mult)
        op("v", ["ka", "kb"], ["ka"], tt, T.ka[:, :], T.ka[:, :], T.kb[:, :], A.add)
        op("v", ["ka"], ["kd"], ts, T.kd[:, :], T.ka[:, :], 1.0, None, A.add)
        op("v", ["kd"], ["kd"], ts, T.kd[:, 15:C:16], T.kd[:, 15:C:16], 2.0 ** -20, None, A.mult)

    def later_copies():
        op("s", [("w0", INP, WEND)], [("w0", OWN, NUM)], act, T.win0[:, OWN:NUM], T.win0[:, INP:WEND], F.Copy)
        op("s", [("w0", INP, WEND)], [("w1", INP, WEND)], act, T.win1[:, INP:WEND], T.win0[:, INP:WEND], F.Copy)

    def product(ps, bank, lc, la, ls, rc, ra, rb, rs, reads):
        op("t", reads, [(ps, bank, bank + 1)], g.tensor.matmul_mx, T[ps][:, 512 * bank:512 * bank + rb - ra], T[lc][:, la:la + 128],
           T[ls][:, la:la + 128], T[rc][:, ra:rb], T[rs][:, ra:rb], True, True)

    sent = 0
    for t in range(R):
        xt, xc, xs, xp = "xt%d" % t, "xc%d" % t, "xs%d" % t, "xp%d" % t
        qx, old, new = "qt%d" % t, "w%d" % (t % 2), "w%d" % ((t + 1) % 2)
        wo, wn = T["win%d" % (t % 2)], T["win%d" % ((t + 1) % 2)]
        for c in range(3):
            product("pc", c, xc, 96 * c, xs, "uc", 0, 128, "us", [qx, "uc"])
        product("pf", 0, "urc", 0, "urs", xc, 0, C, xs, [qx, "urc", "urs"])
        product("pv", 0, "urc", 0, "urs", xc, 0, C, xs, [qx, "urc", "urs"])
        for c in range(3):
            op("v", [("pc", c, c + 1), "low"], [("pmx", c, c + 1)], scan, T.pmx[:, 8 * c:8 * c + 8], T.pc[:, 512 * c:512 * c + 128:16], T.low[:, :], -1e29, A.max, A.max)
        op("v", ["pc"], ["sneg"], ts, T.sneg[:, :], T.pc[:, 1:1536:512], -1.0, None, A.mult)
        op("v", ["pc"], ["cl"], ts, T.cl[:, :], T.pc[:, 2:1536:512], 0.0, None, A.is_gt)
        if t == 0:
            for c in range(3):
                pass
        for c in range(3):
            op("s", [("pmx", c, c + 1)], [("jk", c, c + 1), ("lv", c, c + 1)], act, T.jk[:, 8 * c:8 * c + 8], T.pmx[:, 8 * c:8 * c + 8], F.Sign,
               bias=T.pmx[:, 8 * c + 7:8 * c + 8], scale=-1.0, accum_out=T.lv[:, c:c + 1])
        op("s", ["lv"], ["t1"], act, T.t1[:, :], T.lv[:, :], F.Identity, bias=1024.0, scale=2048.0)
        op("s", ["lv"], ["t3"], act, T.t3[:, :], T.lv[:, :], F.Identity, bias=7454.0, scale=-1024.0)
        for c in range(3):
            op("s", ["pf", "sneg"], [("sg", c, c + 1), ("acc", c, c + 1)], act, T.sg[:, C * c:C * c + C], T.pf[:, 0:C], F.Sign,
               bias=T.sneg[:, c:c + 1], accum_out=T.acc[:, c:c + 1])
        for c in range(3):
            op("v", ["pv", ("pc", c, c + 1)], [("eq", c, c + 1)], ts, T.eq[:, C * c:C * c + C], T.pv[:, 0:C], T.pc[:, 512 * c + 1:512 * c + 2], -1.0, A.is_equal, A.mult)
        op("v", ["t1", "cl"], ["t2"], tt, T.t2[:, :], T.t1[:, :], T.cl[:, :], A.mult)
        for c in range(3):
            op("v", [("eq", c, c + 1), ("kt", c, c + 1)], [("fs", c, c + 1)], scan, T.fs[:, C * c:C * c + C], T.eq[:, C * c:C * c + C],
               T.kt[:, C * c:C * c + C], 0.0, A.add, A.mult)
        op("v", ["t2", "t3"], ["zz"], tt, T.zz[:, :], T.t2[:, :], T.t3[:, :], A.add)
        op("v", ["fs", "zz"], ["wv"], tt, T.wv[:, :], T.fs[:, C - 1:3 * C:C], T.zz[:, :], A.add)
        for c in range(3):
            op("v", ["neg", "wv", ("acc", c, c + 1)], [("bm", c, c + 1)], ts, T.bm[:, 32 * c:32 * c + 32], T.neg[:, :], T.acc[:, c:c + 1], T.wv[:, c:c + 1], A.add, A.add)
        op("v", ["bm"], ["bt"], V.transpose, T.bt[:, :], T.bm[:, :])
        op("v", ["bt", "rm"], ["sc"], scan, T.sc[:, :], T.rm[:, :], T.bt[:, :], 0.0, A.mult, A.max)
        for a in range(3):
            for h in range(2):
                for e, b in (("v", 0), ("s", 1)):
                    o, i = T.glf[32 * b:32 * b + 32, 2 * a + h:18:6], T.sc[32 * a:32 * a + 32, 15 + 16 * h:96:32]
                    w = [("glf", 6 * b + 2 * a + h, 6 * b + 2 * a + h + 1)]
                    if e == "v":
                        op("v", ["sc"], w, cp, o, i)
                    else:
                        op("s", ["sc"], w, act, o, i, F.Copy)
        op("v", [("glf", 0, 12)], [("glf", 12, 24)], cp, T.glf[64:128, :], T.glf[0:64, :])
        op("v", ["glf"], ["gli"], cp, T.gli[:, :], T.glf[:, :])
        op("v", ["gli"], ["rk"], ts, T.rk[:, :], T.gli[:, :], 1, 511, A.logical_shift_right, A.bitwise_and)
        op("v", ["rk"], ["r16"], cp, T.r16[:, :], T.rk[:, :])
        if t == 0:
            later_constants()
            later_copies()
        for k in range(3):
            op("s", ["glf", ("bias", k, k + 1)], [("comp", k, k + 1)], act, T.comp[:, k:72:4], T.glf[:, :], F.Sign, bias=T.bias[:, k:k + 1])
        op("s", ["glf", ("bias", 3, 4)], ["hh"], act, T.hh[:, :], T.glf[:, :], F.Relu, bias=T.bias[:, 3:4], scale=-4.0)
        op("v", ["r16", (old, OWN, NUM)], [(old, 0, C)], cp, wo[:, 0:C].indirect(T.r16[:, 0:18]), wo[:, OWN:NUM])
        op("s", [(old, 0, 1)], [(old, C, C + 1)], act, wo[:, C:C + 1], wo[:, 0:1], F.Copy)
        op("v", ["rk", "hh"], ["ff"], tt, T.ff[:, :], T.hh[:, :], T.rk[:, :], A.add)
        op("v", ["comp", "m4"], ["rest"], scan, T.rest[:, :], T.m4[:, :], T.comp[:, :], 0.0, A.mult, A.add)
        op("v", ["rest", "ff"], ["fm"], tt, T.fm[:, :], T.rest[:, 3:72:4], T.ff[:, :], A.min)
        op("v", ["fm"], ["offd"], ts, T.offd[:, :], T.fm[:, :], 1.0, None, A.add)
        op("v", ["offd", (old, 0, WEND)], [(new, OWN, NUM)], cp, wn[:, OWN:NUM], wo[:, 0:WEND].indirect(T.offd[:, 0:18]))
        op("v", [(new, OWN, NUM), "kd"], ["sk"], scan, T.sk[:, :], wn[:, OWN:NUM], T.kd[:, :], 0.0, A.max, A.mult)
        op("v", ["sk"], ["offz"], ts, T.offz[:, :], T.sk[:, 15:C:16], 1024.0, -1.0, A.mult, A.add)
        zt, zc, zs = "zt%d" % t, "zc%d" % t, "zs%d" % t
        dst = T.cores[(rank + 1 + t) % n]
        rel = relays(core, dst, topo)
        for k, (a, b) in enumerate(PIECE):
            for f in range(4):
                o, i = T[zt][:, 4 * a + f:4 * b:4], T[xp][:, C * f:C * f + C].indirect(T.offz[:, a // 16:b // 16])
                w = [(zt, 4 * k + f, 4 * k + f + 1)]
                if f < 2:
                    op("s", [(xp, f, f + 1), "offz"], w, act, o, i, F.Copy)
                else:
                    op("v", [(xp, f, f + 1), "offz"], w, cp, o, i)
            op("v", [(zt, 4 * k, 4 * k + 4)], [(zc, k, k + 1)], V.quantize_mx, T[zc][:, a:b], T[zs][:, a:b], T[zt][:, 4 * a:4 * b])
            order("g", "out", [(zc, k, k + 1)], [])
            if rel is None:
                sent += send(g, T, topo, core, dst, bits(T["lc%d" % t][:, a:b]), bits(T[zc][:, a:b]), LAND[k] + str(t))
            else:
                sent += send(g, T, topo, core, rel[k], bits(T["rc%d" % t][:, 0:b - a]), bits(T[zc][:, a:b]), "in%d" % t)
        if rel is None:
            sent += send(g, T, topo, core, dst, T["ls%d" % t][:, :], T[zs][:, :], LAND[2] + str(t))
        else:
            sent += send(g, T, topo, core, rel[2], T["rs%d" % t][:, :], T[zs][:, :], "in%d" % t)
        op("v", ["r16", (new, OWN, NUM)], [(new, 0, C)], cp, wn[:, 0:C].indirect(T.r16[:, 0:18]), wn[:, OWN:NUM])
        op("s", [(new, 0, 1)], [(new, C, C + 1)], act, wn[:, C:C + 1], wn[:, 0:1], F.Copy)
        op("v", ["rk"], ["rn16"], ts, T.rn16[:, :], T.rk[:, :], 1.0, None, A.add)
        op("v", ["rn16", (new, 0, OWN)], ["via"], cp, T.via[:, :], wn[:, 0:OWN].indirect(T.rn16[:, 0:18]))
        op("v", ["via", "kd"], ["sk2"], scan, T.sk2[:, :], T.via[:, :], T.kd[:, :], 0.0, A.max, A.mult)
        op("v", ["sk2"], ["offv"], ts, T.offv[:, :], T.sk2[:, 15:C:16], 1024.0, -1.0, A.mult, A.add)
        nx = "xt%d" % (t + 1)
        if t + 1 < R:
            op("v", [], [(nx, 4, 5)], V.memset, T[nx][:, 4 * C:1280], 0.0)
        else:
            op("s", [(new, OWN, NUM)], ["opf"], act, T.opf[:, :], wn[:, OWN:NUM], F.Identity, bias=-1.0)
            load("y", T.op[:, :], T.opf[0:128:16, :], "oop", ["opf"], [])
            op("v", ["vt"], ["vc"], V.quantize_mx, T.vc[:, 0:128], T.vs[:, 0:128], T.vt[:, 0:512])
        src = T.cores[(rank - 1 - t) % n]
        back = relays(src, core, topo)
        for k in range(3):
            w = [("lz%d" % t, k, k + 1)]
            arrived(LAND[k] + str(t), len(topo.engines(src if back is None else back[k], core)), w)
        hs = "hs%d" % t
        for b in range(4):
            product("ph", b % 3, "wcb", 128 * b, "wsb", "lc%d" % t, 0, C, "ls%d" % t, ["lz%d" % t, "wcb", "wsb"])
            op("s", [("ph", b % 3, b % 3 + 1)], [(hs, b, b + 1)], act, T[hs][:, C * b:C * b + C], T.ph[:, 512 * (b % 3):512 * (b % 3) + C], F.Copy, scale=0.00390625)
            op("v", [(hs, b, b + 1), "offv", (xt, b, b + 1)], [(nx, b, b + 1)], tt, T[nx][:, b:4 * C:4], T[hs][:, C * b:C * b + C].indirect(T.offv[:, 0:18]),
               T[xt][:, b:4 * C:4], A.add)
        if t + 1 < R:
            for b in range(4):
                planes(t + 1, b)
            quantise("xc%d" % (t + 1), "xs%d" % (t + 1), nx, 0, 320, "t%d" % (t + 1))
        else:
            quantise("xc3", "xs3", nx, 0, C, "t3")
    load("y", T.oc[:, :], bits(T.xc3[:, 0:C]), "oc", ["qt3"], [])
    product("pf", 0, "vc", 0, "vs", "xc3", 0, CA, "xs3", ["qt3", "vc"])
    product("pv", 0, "vc", 0, "vs", "xc3", CA, C, "xs3", ["qt3", "vc"])
    op("s", ["pf"], [("yt", 0, CA)], act, T.yt[:, 0:CA], T.pf[:, 0:CA], F.Copy)
    op("v", ["pv"], [("yt", CA, C)], cp, T.yt[:, CA:C], T.pv[:, 0:C - CA])
    load("s", T.y[:, 0:CA], T.yt[:, 0:CA], "oy", [("yt", 0, CA)], [])
    load("y", T.y[:, CA:C], T.yt[:, CA:C], "oy2", [("yt", CA, C)], [])
    for k in range(4):
        load("y" if k % 2 else "s", T.osc[4 * k:4 * k + 4, :], T.xs3[32 * k:32 * k + 4, 0:C], "os%d" % k, ["qt3"], [])
    for sem in sorted(cnt):
        need("g", sem, cnt[sem])
    for sem, val in other:
        need("g", sem, val)
    g.wait_ge(T.sem.out, sent)
